import numpy as np
import ml_dtypes


def mxq(x, axis, fmt="e4m3"):
    dtype, down = {"e4m3": (ml_dtypes.float8_e4m3fn, 7), "e5m2": (ml_dtypes.float8_e5m2, 14)}[fmt]
    v = np.moveaxis(np.asarray(x, np.float32).astype(ml_dtypes.bfloat16).astype(np.float64), axis, -1)
    blocks = v.reshape(v.shape[:-1] + (-1, 32))
    amax = np.abs(blocks).max(-1, keepdims=True)
    byte = np.maximum(np.where(amax > 0, np.frexp(amax)[1] - 1 + 127, 0) - down, 1)
    scale = np.exp2(byte - 127.0)
    codes = (blocks / scale).astype(np.float32).astype(dtype).astype(np.float64)
    return np.moveaxis((codes * scale).reshape(v.shape), -1, axis)


WIDE = False


def mx_kscale(k):
    if not WIDE:
        return np.ones(k)
    levels = np.array([10, -10, 5, -5, 0])
    if k % 512:
        return np.exp2(np.random.permutation(np.resize(levels, k // 32))).repeat(32)
    a = np.empty((k // 512, 16))
    for p in range(k // 512):
        a[p, :8] = np.random.permutation(np.resize(levels, 8))
        for g in range(8):
            far = levels[np.abs(levels - a[p, g]) >= 10]
            a[p, g + 8] = far[np.random.randint(len(far))]
    return np.exp2(a.ravel()).repeat(32)


def f64(x):
    return np.asarray(x).astype(np.float64)


def striped(idx):
    return np.tile(idx.reshape(-1, 16).T, (8, 1)).astype(np.uint16)


def unstriped(offs):
    return offs[:16].T.reshape(-1).astype(np.int64)


E2M1 = np.array([0.0, 0.5, 1.0, 1.5, 2.0, 3.0, 4.0, 6.0, -0.0, -0.5, -1.0, -1.5, -2.0, -3.0, -4.0, -6.0])


def pack_fp4(w):
    k, n = w.shape
    w = f64(np.asarray(w, np.float32).astype(ml_dtypes.bfloat16)).reshape(k // 32, 32, n)
    amax = np.abs(w).max(1)
    mant, ex = np.frexp(amax / 6.0)
    byte = np.clip(np.where(amax > 0, np.where(mant > 0.5, ex, ex - 1) + 127, 1), 1, 254)
    scaled = (w * np.exp2(127.0 - byte)[:, None, :]).reshape(k, n).astype(np.float32)
    c = np.ascontiguousarray(scaled.reshape(k // 512, 128, 4, n).transpose(0, 1, 3, 2)).astype(ml_dtypes.float4_e2m1fn).view(np.uint8) & 0xF
    words = (c[..., 0::2] | (c[..., 1::2] << 4)).reshape(k // 512, 128, 2 * n)
    return np.ascontiguousarray(words), np.ascontiguousarray(byte.astype(np.uint8).reshape(k // 512, 16, n))


def unpack_fp4(words, scales):
    g, _, n = scales.shape
    words = np.ascontiguousarray(words).reshape(g, 128, n, 2)
    nib = np.empty((g, 128, n, 4), np.uint8)
    nib[..., 0::2] = words & 0xF
    nib[..., 1::2] = words >> 4
    vals = E2M1[nib] * np.repeat(np.exp2(scales.astype(np.float64) - 127.0), 8, axis=1)[..., None]
    return vals.transpose(0, 1, 3, 2).reshape(g * 512, n)


def gelu(v):
    return 0.5 * v * (1.0 + np.tanh(np.sqrt(2.0 / np.pi) * (v + 0.044715 * v**3)))


K, T, S, H, N = 512, 1024, 512, 512, 128


def setup_inputs():
    n = np.random.standard_normal
    s = mx_kscale(K)[:, None]
    u = mx_kscale(H)
    packed_w2 = pack_fp4(n((H, N)) / np.sqrt(H) / u[:, None])
    return {
        "xT": (n((K, T)) * s).astype(np.float32),
        "w1": (n((K, H)) / np.sqrt(K) / s * u).astype(np.float32),
        "w2_words": packed_w2[0],
        "w2_scales": packed_w2[1],
        "pe": (0.5 * n((H, T)) * u[:, None]).astype(np.float32),
        "offs": striped(np.random.permutation(T)[:S]),
    }


def reference(xT, w1, w2_words, w2_scales, pe, offs):
    xq = mxq(f64(xT)[:, unstriped(offs)], 0, "e4m3")
    g = f64(pe)[:, unstriped(offs)]
    h = gelu((mxq(f64(w1), 0, "e4m3").T @ xq) + g)
    return unpack_fp4(w2_words, w2_scales).T @ mxq(h, 0, "e4m3")

@@ -1,0 +1,180 @@
+from contextlib import ExitStack
+
+import concourse.mybir as mybir
+
+K, T, S, H, N = 512, 1024, 512, 512, 128
+FLOPS = 2 * K * H * S + 2 * H * N * S
+
+F32 = mybir.dt.float32
+BF16 = mybir.dt.bfloat16
+I32 = mybir.dt.int32
+U32 = mybir.dt.uint32
+U16 = mybir.dt.uint16
+U8 = mybir.dt.uint8
+FP8X4 = mybir.dt.float8_e4m3fn_x4
+FP4X4 = mybir.dt.float4_e2m1fn_x4
+GELU = mybir.ActivationFunctionType.Gelu_apprx_tanh
+ADD = mybir.AluOpType.add
+
+P = 128
+PACK = 4
+HALF_T = T // 2
+HALF_M = P // 2
+SCALAR_TOKENS = 192
+SCALAR_CHANNELS = 24
+PIECES = ((0, 128), (128, 256), (256, 384), (384, 512))
+CHUNKS = ((0, 256), (256, 384), (384, 512))
+
+
+def tile_picked_posadd_gelu_l_kernel(tc, xT, w1, w2_words, w2_scales, pe, offs, out):
+    nc = tc.nc
+    with ExitStack() as ctx:
+        keep = ctx.enter_context(tc.tile_pool(name="keep", bufs=1))
+        psum = ctx.enter_context(tc.psum_pool(name="psum", bufs=1))
+
+        warm_in = keep.tile([P, 1], F32, name="warm_in")
+        warm_out = keep.tile([P, 1], F32, name="warm_out")
+        nc.vector.memset(warm_in[:], 0.0)
+        nc.scalar.activation(out=warm_out[:], in_=warm_in[:], func=GELU)
+
+        x_rows = xT.rearrange("(p j) c -> p j c", j=PACK)
+        w1_rows = w1.rearrange("(p j) c -> p j c", j=PACK)
+        pe_rows = pe.rearrange("(p j) c -> p j c", j=PACK)
+
+        offsets = keep.tile([P, S // 16], U16, name="offsets")
+        x_raw = {}
+        for u in range(2):
+            for half in range(2):
+                x_raw[u, half] = keep.tile([P, 2, HALF_T], F32, name="x_raw%d%d" % (u, half))
+                nc.sync.dma_start(
+                    out=x_raw[u, half][:], in_=x_rows[:, 2 * u : 2 * u + 2, half * HALF_T : (half + 1) * HALF_T]
+                )
+            if u == 0:
+                nc.sync.dma_start(offsets[:], offs)
+        w1_raw = []
+        for half in range(2):
+            piece = keep.tile([P, PACK, H // 2], F32, name="w1_raw%d" % half)
+            nc.sync.dma_start(out=piece[:], in_=w1_rows[:, :, half * (H // 2) : (half + 1) * (H // 2)])
+            w1_raw.append(piece)
+        pe_plane = []
+        for t in range(PACK):
+            plane = keep.tile([P, T], F32, name="pe_plane%d" % t)
+            nc.sync.dma_start(out=plane[:], in_=pe_rows[:, t, :])
+            pe_plane.append(plane)
+
+        w2_codes = keep.tile([P, 2 * N], U8, name="w2_codes", align_bytes=64)
+        nc.sync.dma_start(out=w2_codes[:].bitcast(I32), in_=w2_words[0].bitcast(I32))
+        w2_plane = keep.tile([P, N], U8, name="w2_plane", align_bytes=64)
+        nc.gpsimd.memset(w2_plane[:].bitcast(I32), 0)
+        for q in range(4):
+            nc.sync.dma_start(
+                out=w2_plane[32 * q : 32 * q + 4, :].bitcast(I32),
+                in_=w2_scales[0, 4 * q : 4 * q + 4, :].bitcast(I32),
+            )
+
+        x_picked = keep.tile([P, S * PACK], BF16, name="x_picked", align_bytes=64)
+        picked_words = x_picked[:].bitcast(U32).rearrange("p (s u) -> p s u", u=2)
+        for u in range(2):
+            pairs = keep.tile([P, T, 2], BF16, name="pairs%d" % u, align_bytes=64)
+            for copy, half, lo, hi in (
+                (nc.scalar.copy, 0, 0, HALF_T),
+                (nc.scalar.copy, 1, 0, SCALAR_TOKENS),
+                (nc.vector.tensor_copy, 1, SCALAR_TOKENS, HALF_T),
+            ):
+                copy(
+                    out=pairs[:, half * HALF_T + lo : half * HALF_T + hi, :],
+                    in_=x_raw[u, half][:, :, lo:hi].rearrange("p e c -> p c e"),
+                )
+            window = pairs[:].rearrange("p c e -> p (c e)").bitcast(U32)
+            nc.vector.tensor_copy(out=picked_words[:, :, u], in_=window.indirect(offsets[:]))
+
+        x_codes = keep.tile([P, S], U32, name="x_codes", align_bytes=64)
+        x_scales = keep.tile([P, S], U8, name="x_scales", align_bytes=64)
+        nc.vector.quantize_mx(out=x_codes[:].bitcast(FP8X4), scales=x_scales[:], in_=x_picked[:])
+
+        w1_grouped = keep.tile([P, PACK, P, PACK], BF16, name="w1_grouped", align_bytes=64)
+        for copy, half, lo, hi in (
+            (nc.scalar.copy, 0, 0, HALF_M),
+            (nc.scalar.copy, 1, 0, SCALAR_CHANNELS),
+            (nc.vector.tensor_copy, 1, SCALAR_CHANNELS, HALF_M),
+        ):
+            copy(
+                out=w1_grouped[:, :, half * HALF_M + lo : half * HALF_M + hi, :].rearrange("p t m j -> p m j t"),
+                in_=w1_raw[half][:, :, PACK * lo : PACK * hi].rearrange("p j (m t) -> p m j t", t=PACK),
+            )
+        w1_codes = keep.tile([P, H], U32, name="w1_codes", align_bytes=64)
+        w1_scales = keep.tile([P, H], U8, name="w1_scales", align_bytes=64)
+        nc.vector.quantize_mx(
+            out=w1_codes[:].bitcast(FP8X4), scales=w1_scales[:], in_=w1_grouped[:].rearrange("p t m j -> p (t m j)")
+        )
+
+        hidden = {}
+        for t in (1, 0, 2, 3):
+            hidden[t] = psum.tile([P, S], F32, name="hidden%d" % t)
+            rows = slice(t * P, (t + 1) * P)
+            nc.tensor.matmul_mx(
+                out=hidden[t][:],
+                lhsT=w1_codes[:, rows].bitcast(FP8X4),
+                lhsT_scale=w1_scales[:, rows],
+                rhs=x_codes[:].bitcast(FP8X4),
+                rhs_scale=x_scales[:],
+                start=True,
+                stop=True,
+            )
+
+        pe_picked = keep.tile([P, S], F32, name="pe_picked")
+        nc.vector.tensor_copy(out=pe_picked[:], in_=pe_plane[0][:].indirect(offsets[:]))
+        product = {}
+        for t in range(1, PACK):
+            product[t] = keep.tile([P, S], F32, name="product%d" % t)
+            nc.scalar.copy(out=product[t][:], in_=hidden[t][:])
+
+        summed = [keep.tile([P, 2, S], F32, name="summed%d" % u) for u in range(2)]
+        h_grouped = keep.tile([P, S, PACK], BF16, name="h_grouped", align_bytes=64)
+
+        def gather_add(t, lo, hi):
+            nc.vector.tensor_tensor(
+                out=summed[t // 2][:, t % 2, lo:hi],
+                in0=pe_plane[t][:].indirect(offsets[:, lo // 16 : hi // 16]),
+                in1=product[t][:, lo:hi],
+                op=ADD,
+            )
+
+        def gelu_pair(u, lo, hi):
+            nc.scalar.activation(
+                out=h_grouped[:, lo:hi, 2 * u : 2 * u + 2],
+                in_=summed[u][:, :, lo:hi].rearrange("p e s -> p s e"),
+                func=GELU,
+            )
+
+        def second_layer(lo, hi):
+            h_codes = keep.tile([P, hi - lo], U32, name="h_codes%d" % lo, align_bytes=64)
+            h_scales = keep.tile([P, hi - lo], U8, name="h_scales%d" % lo, align_bytes=64)
+            nc.vector.quantize_mx(
+                out=h_codes[:].bitcast(FP8X4),
+                scales=h_scales[:],
+                in_=h_grouped[:, lo:hi, :].rearrange("p s t -> p (s t)"),
+            )
+            acc = psum.tile([P, hi - lo], F32, name="acc%d" % lo)
+            nc.tensor.matmul_mx(
+                out=acc[:],
+                lhsT=w2_codes[:].bitcast(FP4X4),
+                lhsT_scale=w2_plane[:],
+                rhs=h_codes[:].bitcast(FP8X4),
+                rhs_scale=h_scales[:],
+                start=True,
+                stop=True,
+            )
+            result = keep.tile([P, hi - lo], F32, name="result%d" % lo)
+            nc.vector.tensor_copy(out=result[:], in_=acc[:])
+            nc.sync.dma_start(out=out[:, lo:hi], in_=result[:])
+
+        nc.vector.tensor_tensor(out=summed[0][:, 0, :], in0=hidden[0][:], in1=pe_picked[:], op=ADD)
+        gather_add(1, 0, S)
+        gelu_pair(0, 0, S)
+        gather_add(2, 0, S)
+        for lo, hi in PIECES:
+            gather_add(3, lo, hi)
+            gelu_pair(1, lo, hi)
+        for lo, hi in CHUNKS:
+            second_layer(lo, hi)

@@ -20,10 +20,10 @@ P = 128
 PACK = 4
 HALF_T = T // 2
 HALF_M = P // 2
-SCALAR_TOKENS = 192
-SCALAR_CHANNELS = 24
-PIECES = ((0, 128), (128, 256), (256, 384), (384, 512))
-CHUNKS = ((0, 256), (256, 384), (384, 512))
+SCALAR_TOKENS = 256
+SCALAR_CHANNELS = 40
+EARLY = 0
+PLAIN = 1
 
 
 def tile_picked_posadd_gelu_l_kernel(tc, xT, w1, w2_words, w2_scales, pe, offs, out):
@@ -51,16 +51,17 @@ def tile_picked_posadd_gelu_l_kernel(tc, xT, w1, w2_words, w2_scales, pe, offs, 
                 )
             if u == 0:
                 nc.sync.dma_start(offsets[:], offs)
-        w1_raw = []
+        pe_plane = [keep.tile([P, T], F32, name="pe_plane%d" % t) for t in range(PACK)]
+        w1_raw = [
+            keep.tile([P, PACK, H // 2], F32, name="w1_raw%d" % half, tag=tag, align_bytes=64)
+            for half, tag in enumerate(("w1_first", "w1_second"))
+        ]
+        for t in range(EARLY):
+            nc.sync.dma_start(out=pe_plane[t][:], in_=pe_rows[:, t, :])
         for half in range(2):
-            piece = keep.tile([P, PACK, H // 2], F32, name="w1_raw%d" % half)
-            nc.sync.dma_start(out=piece[:], in_=w1_rows[:, :, half * (H // 2) : (half + 1) * (H // 2)])
-            w1_raw.append(piece)
-        pe_plane = []
-        for t in range(PACK):
-            plane = keep.tile([P, T], F32, name="pe_plane%d" % t)
-            nc.sync.dma_start(out=plane[:], in_=pe_rows[:, t, :])
-            pe_plane.append(plane)
+            nc.sync.dma_start(out=w1_raw[half][:], in_=w1_rows[:, :, half * (H // 2) : (half + 1) * (H // 2)])
+        for t in range(EARLY, PACK):
+            nc.sync.dma_start(out=pe_plane[t][:], in_=pe_rows[:, t, :])
 
         w2_codes = keep.tile([P, 2 * N], U8, name="w2_codes", align_bytes=64)
         nc.sync.dma_start(out=w2_codes[:].bitcast(I32), in_=w2_words[0].bitcast(I32))
@@ -88,10 +89,9 @@ def tile_picked_posadd_gelu_l_kernel(tc, xT, w1, w2_words, w2_scales, pe, offs, 
             window = pairs[:].rearrange("p c e -> p (c e)").bitcast(U32)
             nc.vector.tensor_copy(out=picked_words[:, :, u], in_=window.indirect(offsets[:]))
 
-        x_codes = keep.tile([P, S], U32, name="x_codes", align_bytes=64)
-        x_scales = keep.tile([P, S], U8, name="x_scales", align_bytes=64)
-        nc.vector.quantize_mx(out=x_codes[:].bitcast(FP8X4), scales=x_scales[:], in_=x_picked[:])
-
+        pe_picked = keep.tile([P, PLAIN, S], F32, name="pe_picked")
+        for t in range(EARLY):
+            nc.vector.tensor_copy(out=pe_picked[:, t, :], in_=pe_plane[t][:].indirect(offsets[:]))
         w1_grouped = keep.tile([P, PACK, P, PACK], BF16, name="w1_grouped", align_bytes=64)
         for copy, half, lo, hi in (
             (nc.scalar.copy, 0, 0, HALF_M),
@@ -102,14 +102,22 @@ def tile_picked_posadd_gelu_l_kernel(tc, xT, w1, w2_words, w2_scales, pe, offs, 
                 out=w1_grouped[:, :, half * HALF_M + lo : half * HALF_M + hi, :].rearrange("p t m j -> p m j t"),
                 in_=w1_raw[half][:, :, PACK * lo : PACK * hi].rearrange("p j (m t) -> p m j t", t=PACK),
             )
+        x_codes = keep.tile([P, S], U32, name="x_codes", tag="w1_first", align_bytes=64)
+        x_scales = keep.tile([P, S], U8, name="x_scales", align_bytes=64)
+        nc.vector.quantize_mx(out=x_codes[:].bitcast(FP8X4), scales=x_scales[:], in_=x_picked[:])
+
         w1_codes = keep.tile([P, H], U32, name="w1_codes", align_bytes=64)
         w1_scales = keep.tile([P, H], U8, name="w1_scales", align_bytes=64)
-        nc.vector.quantize_mx(
-            out=w1_codes[:].bitcast(FP8X4), scales=w1_scales[:], in_=w1_grouped[:].rearrange("p t m j -> p (t m j)")
-        )
+        for u in range(2):
+            cols = slice(2 * u * P, (2 * u + 2) * P)
+            nc.vector.quantize_mx(
+                out=w1_codes[:, cols].bitcast(FP8X4),
+                scales=w1_scales[:, cols],
+                in_=w1_grouped[:, 2 * u : 2 * u + 2, :, :].rearrange("p t m j -> p (t m j)"),
+            )
 
         hidden = {}
-        for t in (1, 0, 2, 3):
+        for t in (1, 2, 0, 3):
             hidden[t] = psum.tile([P, S], F32, name="hidden%d" % t)
             rows = slice(t * P, (t + 1) * P)
             nc.tensor.matmul_mx(
@@ -122,19 +130,19 @@ def tile_picked_posadd_gelu_l_kernel(tc, xT, w1, w2_words, w2_scales, pe, offs, 
                 stop=True,
             )
 
-        pe_picked = keep.tile([P, S], F32, name="pe_picked")
-        nc.vector.tensor_copy(out=pe_picked[:], in_=pe_plane[0][:].indirect(offsets[:]))
+        for t in range(EARLY, PLAIN):
+            nc.vector.tensor_copy(out=pe_picked[:, t, :], in_=pe_plane[t][:].indirect(offsets[:]))
         product = {}
-        for t in range(1, PACK):
+        for t in range(PLAIN, PACK):
             product[t] = keep.tile([P, S], F32, name="product%d" % t)
             nc.scalar.copy(out=product[t][:], in_=hidden[t][:])
 
-        summed = [keep.tile([P, 2, S], F32, name="summed%d" % u) for u in range(2)]
+        summed = keep.tile([P, PACK, S], F32, name="summed")
         h_grouped = keep.tile([P, S, PACK], BF16, name="h_grouped", align_bytes=64)
 
         def gather_add(t, lo, hi):
             nc.vector.tensor_tensor(
-                out=summed[t // 2][:, t % 2, lo:hi],
+                out=summed[:, t, lo:hi],
                 in0=pe_plane[t][:].indirect(offsets[:, lo // 16 : hi // 16]),
                 in1=product[t][:, lo:hi],
                 op=ADD,
@@ -143,11 +151,21 @@ def tile_picked_posadd_gelu_l_kernel(tc, xT, w1, w2_words, w2_scales, pe, offs, 
         def gelu_pair(u, lo, hi):
             nc.scalar.activation(
                 out=h_grouped[:, lo:hi, 2 * u : 2 * u + 2],
-                in_=summed[u][:, :, lo:hi].rearrange("p e s -> p s e"),
+                in_=summed[:, 2 * u : 2 * u + 2, lo:hi].rearrange("p e s -> p s e"),
                 func=GELU,
             )
 
-        def second_layer(lo, hi):
+        def gelu_quad(lo, hi):
+            nc.scalar.activation(
+                out=h_grouped[:, lo:hi, :].rearrange("p (g i) t -> p g t i", i=4),
+                in_=summed[:, :, lo:hi].rearrange("p t (g i) -> p g t i", i=4),
+                func=GELU,
+            )
+
+        def plain_add(t, lo, hi):
+            nc.vector.tensor_tensor(out=summed[:, t, lo:hi], in0=hidden[t][:, lo:hi], in1=pe_picked[:, t, lo:hi], op=ADD)
+
+        def second_layer(lo, hi, copy):
             h_codes = keep.tile([P, hi - lo], U32, name="h_codes%d" % lo, align_bytes=64)
             h_scales = keep.tile([P, hi - lo], U8, name="h_scales%d" % lo, align_bytes=64)
             nc.vector.quantize_mx(
@@ -166,15 +184,19 @@ def tile_picked_posadd_gelu_l_kernel(tc, xT, w1, w2_words, w2_scales, pe, offs, 
                 stop=True,
             )
             result = keep.tile([P, hi - lo], F32, name="result%d" % lo)
-            nc.vector.tensor_copy(out=result[:], in_=acc[:])
+            copy(out=result[:], in_=acc[:])
             nc.sync.dma_start(out=out[:, lo:hi], in_=result[:])
 
-        nc.vector.tensor_tensor(out=summed[0][:, 0, :], in0=hidden[0][:], in1=pe_picked[:], op=ADD)
         gather_add(1, 0, S)
-        gelu_pair(0, 0, S)
-        gather_add(2, 0, S)
-        for lo, hi in PIECES:
-            gather_add(3, lo, hi)
-            gelu_pair(1, lo, hi)
-        for lo, hi in CHUNKS:
-            second_layer(lo, hi)
+        plain_add(0, 0, S)
+        gelu_pair(0, 128, S)
+        gather_add(2, 0, 128)
+        gather_add(3, 0, 128)
+        gelu_quad(0, 128)
+        gather_add(2, 128, S)
+        for lo in range(128, S, 128):
+            gather_add(3, lo, lo + 128)
+            gelu_pair(1, lo, lo + 128)
+        second_layer(0, 256, nc.scalar.copy)
+        second_layer(256, 384, nc.scalar.copy)
+        second_layer(384, 512, nc.vector.tensor_copy)

@@ -18,12 +18,12 @@ ADD = mybir.AluOpType.add
 
 P = 128
 PACK = 4
+HALF_S = S // 2
+CHUNK = 128
 HALF_T = T // 2
 HALF_M = P // 2
 SCALAR_TOKENS = 256
 SCALAR_CHANNELS = 40
-EARLY = 0
-PLAIN = 1
 
 
 def tile_picked_posadd_gelu_l_kernel(tc, xT, w1, w2_words, w2_scales, pe, offs, out):
@@ -51,16 +51,14 @@ def tile_picked_posadd_gelu_l_kernel(tc, xT, w1, w2_words, w2_scales, pe, offs, 
                 )
             if u == 0:
                 nc.sync.dma_start(offsets[:], offs)
-        pe_plane = [keep.tile([P, T], F32, name="pe_plane%d" % t) for t in range(PACK)]
+        pe_plane = [keep.tile([P, T], F32, name="pe_plane%d" % t, align_bytes=64) for t in range(PACK)]
         w1_raw = [
             keep.tile([P, PACK, H // 2], F32, name="w1_raw%d" % half, tag=tag, align_bytes=64)
             for half, tag in enumerate(("w1_first", "w1_second"))
         ]
-        for t in range(EARLY):
-            nc.sync.dma_start(out=pe_plane[t][:], in_=pe_rows[:, t, :])
         for half in range(2):
             nc.sync.dma_start(out=w1_raw[half][:], in_=w1_rows[:, :, half * (H // 2) : (half + 1) * (H // 2)])
-        for t in range(EARLY, PACK):
+        for t in range(PACK):
             nc.sync.dma_start(out=pe_plane[t][:], in_=pe_rows[:, t, :])
 
         w2_codes = keep.tile([P, 2 * N], U8, name="w2_codes", align_bytes=64)
@@ -89,9 +87,6 @@ def tile_picked_posadd_gelu_l_kernel(tc, xT, w1, w2_words, w2_scales, pe, offs, 
             window = pairs[:].rearrange("p c e -> p (c e)").bitcast(U32)
             nc.vector.tensor_copy(out=picked_words[:, :, u], in_=window.indirect(offsets[:]))
 
-        pe_picked = keep.tile([P, PLAIN, S], F32, name="pe_picked")
-        for t in range(EARLY):
-            nc.vector.tensor_copy(out=pe_picked[:, t, :], in_=pe_plane[t][:].indirect(offsets[:]))
         w1_grouped = keep.tile([P, PACK, P, PACK], BF16, name="w1_grouped", align_bytes=64)
         for copy, half, lo, hi in (
             (nc.scalar.copy, 0, 0, HALF_M),
@@ -117,7 +112,7 @@ def tile_picked_posadd_gelu_l_kernel(tc, xT, w1, w2_words, w2_scales, pe, offs, 
             )
 
         hidden = {}
-        for t in (1, 2, 0, 3):
+        for t in (1, 0, 2, 3):
             hidden[t] = psum.tile([P, S], F32, name="hidden%d" % t)
             rows = slice(t * P, (t + 1) * P)
             nc.tensor.matmul_mx(
@@ -130,28 +125,37 @@ def tile_picked_posadd_gelu_l_kernel(tc, xT, w1, w2_words, w2_scales, pe, offs, 
                 stop=True,
             )
 
-        for t in range(EARLY, PLAIN):
-            nc.vector.tensor_copy(out=pe_picked[:, t, :], in_=pe_plane[t][:].indirect(offsets[:]))
-        product = {}
-        for t in range(PLAIN, PACK):
-            product[t] = keep.tile([P, S], F32, name="product%d" % t)
-            nc.scalar.copy(out=product[t][:], in_=hidden[t][:])
-
+        pe_picked = keep.tile([P, S], F32, name="pe_picked")
+        nc.vector.tensor_copy(out=pe_picked[:], in_=pe_plane[0][:].indirect(offsets[:]))
+        late = keep.tile([P, 2 * (CHUNK + S)], F32, name="late")
         summed = keep.tile([P, PACK, S], F32, name="summed")
+        product = {
+            (1, 0): summed[:, 0, 0:HALF_S],
+            (1, 1): keep.tile([P, HALF_S], F32, name="product1")[:],
+        }
+        for half in range(2):
+            nc.scalar.copy(out=product[1, half], in_=hidden[1][:, half * HALF_S : (half + 1) * HALF_S])
+        whole = {2: keep.tile([P, S], F32, name="product2")[:], 3: late[:, CHUNK : CHUNK + S]}
+        for t in (2, 3):
+            nc.scalar.copy(out=whole[t], in_=hidden[t][:])
+            for half in range(2):
+                product[t, half] = whole[t][:, half * HALF_S : (half + 1) * HALF_S]
+
+        late_sums = late[:].rearrange("p (e s) -> p e s", e=2)[:, :, 0:HALF_S]
         h_grouped = keep.tile([P, S, PACK], BF16, name="h_grouped", align_bytes=64)
 
-        def gather_add(t, lo, hi):
+        def gather_add(t, lo, hi, sums):
             nc.vector.tensor_tensor(
-                out=summed[:, t, lo:hi],
+                out=sums,
                 in0=pe_plane[t][:].indirect(offsets[:, lo // 16 : hi // 16]),
-                in1=product[t][:, lo:hi],
+                in1=product[t, lo // HALF_S][:, lo % HALF_S : lo % HALF_S + hi - lo],
                 op=ADD,
             )
 
-        def gelu_pair(u, lo, hi):
+        def gelu_pair(u, lo, hi, sums):
             nc.scalar.activation(
                 out=h_grouped[:, lo:hi, 2 * u : 2 * u + 2],
-                in_=summed[:, 2 * u : 2 * u + 2, lo:hi].rearrange("p e s -> p s e"),
+                in_=sums.rearrange("p e s -> p s e"),
                 func=GELU,
             )
 
@@ -162,15 +166,29 @@ def tile_picked_posadd_gelu_l_kernel(tc, xT, w1, w2_words, w2_scales, pe, offs, 
                 func=GELU,
             )
 
-        def plain_add(t, lo, hi):
-            nc.vector.tensor_tensor(out=summed[:, t, lo:hi], in0=hidden[t][:, lo:hi], in1=pe_picked[:, t, lo:hi], op=ADD)
+        for lo in range(0, S, HALF_S):
+            gather_add(1, lo, lo + HALF_S, summed[:, 1, lo : lo + HALF_S])
+        nc.vector.tensor_tensor(out=summed[:, 0, :], in0=hidden[0][:], in1=pe_picked[:], op=ADD)
+        gelu_pair(0, HALF_S, S, summed[:, 0:2, HALF_S:S])
+        gather_add(2, 0, HALF_S, summed[:, 2, 0:HALF_S])
+        for lo in range(0, HALF_S, CHUNK):
+            gather_add(3, lo, lo + CHUNK, summed[:, 3, lo : lo + CHUNK])
+            gelu_quad(lo, lo + CHUNK)
+        gather_add(2, HALF_S, S, late_sums[:, 0, :])
+        for lo in range(0, HALF_S, CHUNK):
+            gather_add(3, HALF_S + lo, HALF_S + lo + CHUNK, late_sums[:, 1, lo : lo + CHUNK])
+            gelu_pair(1, HALF_S + lo, HALF_S + lo + CHUNK, late_sums[:, :, lo : lo + CHUNK])
 
-        def second_layer(lo, hi, copy):
-            h_codes = keep.tile([P, hi - lo], U32, name="h_codes%d" % lo, align_bytes=64)
-            h_scales = keep.tile([P, hi - lo], U8, name="h_scales%d" % lo, align_bytes=64)
+        h_codes = keep.tile([P, S], U32, name="h_codes", tag="pe_plane2", align_bytes=64)
+        h_scales = keep.tile([P, S], U8, name="h_scales", align_bytes=64)
+        for lo, hi, copy in (
+            (0, 256, nc.scalar.copy),
+            (256, 384, nc.scalar.copy),
+            (384, 512, nc.vector.tensor_copy),
+        ):
             nc.vector.quantize_mx(
-                out=h_codes[:].bitcast(FP8X4),
-                scales=h_scales[:],
+                out=h_codes[:, lo:hi].bitcast(FP8X4),
+                scales=h_scales[:, lo:hi],
                 in_=h_grouped[:, lo:hi, :].rearrange("p s t -> p (s t)"),
             )
             acc = psum.tile([P, hi - lo], F32, name="acc%d" % lo)
@@ -178,25 +196,11 @@ def tile_picked_posadd_gelu_l_kernel(tc, xT, w1, w2_words, w2_scales, pe, offs, 
                 out=acc[:],
                 lhsT=w2_codes[:].bitcast(FP4X4),
                 lhsT_scale=w2_plane[:],
-                rhs=h_codes[:].bitcast(FP8X4),
-                rhs_scale=h_scales[:],
+                rhs=h_codes[:, lo:hi].bitcast(FP8X4),
+                rhs_scale=h_scales[:, lo:hi],
                 start=True,
                 stop=True,
             )
             result = keep.tile([P, hi - lo], F32, name="result%d" % lo)
             copy(out=result[:], in_=acc[:])
             nc.sync.dma_start(out=out[:, lo:hi], in_=result[:])
-
-        gather_add(1, 0, S)
-        plain_add(0, 0, S)
-        gelu_pair(0, 128, S)
-        gather_add(2, 0, 128)
-        gather_add(3, 0, 128)
-        gelu_quad(0, 128)
-        gather_add(2, 128, S)
-        for lo in range(128, S, 128):
-            gather_add(3, lo, lo + 128)
-            gelu_pair(1, lo, lo + 128)
-        second_layer(0, 256, nc.scalar.copy)
-        second_layer(256, 384, nc.scalar.copy)
-        second_layer(384, 512, nc.vector.tensor_copy)

@@ -20,9 +20,7 @@ P = 128
 PACK = 4
 HALF_S = S // 2
 CHUNK = 128
-HALF_T = T // 2
 HALF_M = P // 2
-SCALAR_TOKENS = 256
 SCALAR_CHANNELS = 40
 
 
@@ -42,15 +40,10 @@ def tile_picked_posadd_gelu_l_kernel(tc, xT, w1, w2_words, w2_scales, pe, offs, 
         pe_rows = pe.rearrange("(p j) c -> p j c", j=PACK)
 
         offsets = keep.tile([P, S // 16], U16, name="offsets")
-        x_raw = {}
-        for u in range(2):
-            for half in range(2):
-                x_raw[u, half] = keep.tile([P, 2, HALF_T], F32, name="x_raw%d%d" % (u, half))
-                nc.sync.dma_start(
-                    out=x_raw[u, half][:], in_=x_rows[:, 2 * u : 2 * u + 2, half * HALF_T : (half + 1) * HALF_T]
-                )
-            if u == 0:
-                nc.sync.dma_start(offsets[:], offs)
+        nc.sync.dma_start(offsets[:], offs)
+        x_plane = [keep.tile([P, T], F32, name="x_plane%d" % j) for j in range(PACK)]
+        for j in range(PACK):
+            nc.sync.dma_start(out=x_plane[j][:], in_=x_rows[:, j, :])
         pe_plane = [keep.tile([P, T], F32, name="pe_plane%d" % t, align_bytes=64) for t in range(PACK)]
         w1_raw = [
             keep.tile([P, PACK, H // 2], F32, name="w1_raw%d" % half, tag=tag, align_bytes=64)
@@ -71,21 +64,25 @@ def tile_picked_posadd_gelu_l_kernel(tc, xT, w1, w2_words, w2_scales, pe, offs, 
                 in_=w2_scales[0, 4 * q : 4 * q + 4, :].bitcast(I32),
             )
 
-        x_picked = keep.tile([P, S * PACK], BF16, name="x_picked", align_bytes=64)
-        picked_words = x_picked[:].bitcast(U32).rearrange("p (s u) -> p s u", u=2)
-        for u in range(2):
-            pairs = keep.tile([P, T, 2], BF16, name="pairs%d" % u, align_bytes=64)
-            for copy, half, lo, hi in (
-                (nc.scalar.copy, 0, 0, HALF_T),
-                (nc.scalar.copy, 1, 0, SCALAR_TOKENS),
-                (nc.vector.tensor_copy, 1, SCALAR_TOKENS, HALF_T),
-            ):
-                copy(
-                    out=pairs[:, half * HALF_T + lo : half * HALF_T + hi, :],
-                    in_=x_raw[u, half][:, :, lo:hi].rearrange("p e c -> p c e"),
-                )
-            window = pairs[:].rearrange("p c e -> p (c e)").bitcast(U32)
-            nc.vector.tensor_copy(out=picked_words[:, :, u], in_=window.indirect(offsets[:]))
+        x_found = keep.tile([P, PACK, S], F32, name="x_found")
+        x_picked = keep.tile([P, S, PACK], BF16, name="x_picked", align_bytes=64)
+
+        def gather_x(j, lo, hi):
+            nc.vector.tensor_copy(out=x_found[:, j, lo:hi], in_=x_plane[j][:].indirect(offsets[:, lo // 16 : hi // 16]))
+
+        def weave_x(copy, u, lo, hi):
+            copy(
+                out=x_picked[:, lo:hi, 2 * u : 2 * u + 2],
+                in_=x_found[:, 2 * u : 2 * u + 2, lo:hi].rearrange("p e s -> p s e"),
+            )
+
+        for j in range(PACK - 1):
+            gather_x(j, 0, S)
+        weave_x(nc.scalar.copy, 0, 0, S)
+        for lo in range(0, S, HALF_S):
+            gather_x(PACK - 1, lo, lo + HALF_S)
+        for lo in range(0, S, HALF_S):
+            weave_x(nc.vector.tensor_copy, 1, lo, lo + HALF_S)
 
         w1_grouped = keep.tile([P, PACK, P, PACK], BF16, name="w1_grouped", align_bytes=64)
         for copy, half, lo, hi in (
@@ -99,7 +96,7 @@ def tile_picked_posadd_gelu_l_kernel(tc, xT, w1, w2_words, w2_scales, pe, offs, 
             )
         x_codes = keep.tile([P, S], U32, name="x_codes", tag="w1_first", align_bytes=64)
         x_scales = keep.tile([P, S], U8, name="x_scales", align_bytes=64)
-        nc.vector.quantize_mx(out=x_codes[:].bitcast(FP8X4), scales=x_scales[:], in_=x_picked[:])
+        nc.vector.quantize_mx(out=x_codes[:].bitcast(FP8X4), scales=x_scales[:], in_=x_picked[:].rearrange("p s j -> p (s j)"))
 
         w1_codes = keep.tile([P, H], U32, name="w1_codes", align_bytes=64)
         w1_scales = keep.tile([P, H], U8, name="w1_scales", align_bytes=64)

@@ -14,6 +14,7 @@ U8 = mybir.dt.uint8
 FP8X4 = mybir.dt.float8_e4m3fn_x4
 FP4X4 = mybir.dt.float4_e2m1fn_x4
 GELU = mybir.ActivationFunctionType.Gelu_apprx_tanh
+COPY = mybir.ActivationFunctionType.Copy
 ADD = mybir.AluOpType.add
 
 P = 128
@@ -64,25 +65,21 @@ def tile_picked_posadd_gelu_l_kernel(tc, xT, w1, w2_words, w2_scales, pe, offs, 
                 in_=w2_scales[0, 4 * q : 4 * q + 4, :].bitcast(I32),
             )
 
-        x_found = keep.tile([P, PACK, S], F32, name="x_found")
         x_picked = keep.tile([P, S, PACK], BF16, name="x_picked", align_bytes=64)
-
-        def gather_x(j, lo, hi):
-            nc.vector.tensor_copy(out=x_found[:, j, lo:hi], in_=x_plane[j][:].indirect(offsets[:, lo // 16 : hi // 16]))
-
-        def weave_x(copy, u, lo, hi):
-            copy(
-                out=x_picked[:, lo:hi, 2 * u : 2 * u + 2],
-                in_=x_found[:, 2 * u : 2 * u + 2, lo:hi].rearrange("p e s -> p s e"),
+        for j in range(2):
+            rounded = keep.tile([P, T], BF16, name="x_rounded%d" % j)
+            nc.vector.tensor_copy(out=rounded[:], in_=x_plane[j][:])
+            nc.scalar.activation(out=x_picked[:, :, j], in_=rounded[:].indirect(offsets[:]), func=COPY)
+        x_found = keep.tile([P, 2, S], F32, name="x_found")
+        for j, lo, hi in ((2, 0, S), (3, 0, HALF_S), (3, HALF_S, S)):
+            nc.vector.tensor_copy(
+                out=x_found[:, j - 2, lo:hi], in_=x_plane[j][:].indirect(offsets[:, lo // 16 : hi // 16])
             )
-
-        for j in range(PACK - 1):
-            gather_x(j, 0, S)
-        weave_x(nc.scalar.copy, 0, 0, S)
         for lo in range(0, S, HALF_S):
-            gather_x(PACK - 1, lo, lo + HALF_S)
-        for lo in range(0, S, HALF_S):
-            weave_x(nc.vector.tensor_copy, 1, lo, lo + HALF_S)
+            nc.vector.tensor_copy(
+                out=x_picked[:, lo : lo + HALF_S, 2:4],
+                in_=x_found[:, :, lo : lo + HALF_S].rearrange("p e s -> p s e"),
+            )
 
         w1_grouped = keep.tile([P, PACK, P, PACK], BF16, name="w1_grouped", align_bytes=64)
         for copy, half, lo, hi in (

@@ -14,7 +14,7 @@ U8 = mybir.dt.uint8
 FP8X4 = mybir.dt.float8_e4m3fn_x4
 FP4X4 = mybir.dt.float4_e2m1fn_x4
 GELU = mybir.ActivationFunctionType.Gelu_apprx_tanh
-COPY = mybir.ActivationFunctionType.Copy
+MULT = mybir.AluOpType.mult
 ADD = mybir.AluOpType.add
 
 P = 128
@@ -66,20 +66,41 @@ def tile_picked_posadd_gelu_l_kernel(tc, xT, w1, w2_words, w2_scales, pe, offs, 
             )
 
         x_picked = keep.tile([P, S, PACK], BF16, name="x_picked", align_bytes=64)
-        for j in range(2):
-            rounded = keep.tile([P, T], BF16, name="x_rounded%d" % j)
-            nc.vector.tensor_copy(out=rounded[:], in_=x_plane[j][:])
-            nc.scalar.activation(out=x_picked[:, :, j], in_=rounded[:].indirect(offsets[:]), func=COPY)
-        x_found = keep.tile([P, 2, S], F32, name="x_found")
-        for j, lo, hi in ((2, 0, S), (3, 0, HALF_S), (3, HALF_S, S)):
-            nc.vector.tensor_copy(
-                out=x_found[:, j - 2, lo:hi], in_=x_plane[j][:].indirect(offsets[:, lo // 16 : hi // 16])
+        x_found = keep.tile([P, PACK, S], F32, name="x_found")
+
+        def gather_x(j, lo, hi):
+            nc.vector.tensor_copy(out=x_found[:, j, lo:hi], in_=x_plane[j][:].indirect(offsets[:, lo // 16 : hi // 16]))
+
+        def gpsimd_copy(out, in_):
+            nc.gpsimd.tensor_scalar(out, in_, 1.0, 0.0, MULT, ADD)
+
+        def weave_x(copy, u, lo, hi):
+            copy(
+                out=x_picked[:, lo:hi, 2 * u : 2 * u + 2],
+                in_=x_found[:, 2 * u : 2 * u + 2, lo:hi].rearrange("p e s -> p s e"),
             )
-        for lo in range(0, S, HALF_S):
-            nc.vector.tensor_copy(
-                out=x_picked[:, lo : lo + HALF_S, 2:4],
-                in_=x_found[:, :, lo : lo + HALF_S].rearrange("p e s -> p s e"),
+
+        for j in range(PACK - 1):
+            gather_x(j, 0, S)
+        weave_x(nc.scalar.copy, 0, 0, S)
+        pieces = ((gpsimd_copy, 0, 160), (nc.vector.tensor_copy, 160, HALF_S), (nc.vector.tensor_copy, HALF_S, S))
+        for lo, hi in ((0, 160), (160, 320), (320, S)):
+            gather_x(PACK - 1, lo, hi)
+        for copy, lo, hi in pieces:
+            weave_x(copy, 1, lo, hi)
+
+        x_codes = {}
+        x_scales = keep.tile([P, S], U8, name="x_scales", align_bytes=64)
+
+        def quantize_x(lo, tag):
+            x_codes[lo] = keep.tile([P, HALF_S], U32, name="x_codes%d" % lo, tag=tag, align_bytes=64)
+            nc.vector.quantize_mx(
+                out=x_codes[lo][:].bitcast(FP8X4),
+                scales=x_scales[:, lo : lo + HALF_S],
+                in_=x_picked[:, lo : lo + HALF_S, :].rearrange("p s j -> p (s j)"),
             )
+
+        quantize_x(0, "x_codes0")
 
         w1_grouped = keep.tile([P, PACK, P, PACK], BF16, name="w1_grouped", align_bytes=64)
         for copy, half, lo, hi in (
@@ -91,9 +112,7 @@ def tile_picked_posadd_gelu_l_kernel(tc, xT, w1, w2_words, w2_scales, pe, offs, 
                 out=w1_grouped[:, :, half * HALF_M + lo : half * HALF_M + hi, :].rearrange("p t m j -> p m j t"),
                 in_=w1_raw[half][:, :, PACK * lo : PACK * hi].rearrange("p j (m t) -> p m j t", t=PACK),
             )
-        x_codes = keep.tile([P, S], U32, name="x_codes", tag="w1_first", align_bytes=64)
-        x_scales = keep.tile([P, S], U8, name="x_scales", align_bytes=64)
-        nc.vector.quantize_mx(out=x_codes[:].bitcast(FP8X4), scales=x_scales[:], in_=x_picked[:].rearrange("p s j -> p (s j)"))
+        quantize_x(HALF_S, "w1_first")
 
         w1_codes = keep.tile([P, H], U32, name="w1_codes", align_bytes=64)
         w1_scales = keep.tile([P, H], U8, name="w1_scales", align_bytes=64)
@@ -109,15 +128,16 @@ def tile_picked_posadd_gelu_l_kernel(tc, xT, w1, w2_words, w2_scales, pe, offs, 
         for t in (1, 0, 2, 3):
             hidden[t] = psum.tile([P, S], F32, name="hidden%d" % t)
             rows = slice(t * P, (t + 1) * P)
-            nc.tensor.matmul_mx(
-                out=hidden[t][:],
-                lhsT=w1_codes[:, rows].bitcast(FP8X4),
-                lhsT_scale=w1_scales[:, rows],
-                rhs=x_codes[:].bitcast(FP8X4),
-                rhs_scale=x_scales[:],
-                start=True,
-                stop=True,
-            )
+            for lo in range(0, S, HALF_S):
+                nc.tensor.matmul_mx(
+                    out=hidden[t][:, lo : lo + HALF_S],
+                    lhsT=w1_codes[:, rows].bitcast(FP8X4),
+                    lhsT_scale=w1_scales[:, rows],
+                    rhs=x_codes[lo][:].bitcast(FP8X4),
+                    rhs_scale=x_scales[:, lo : lo + HALF_S],
+                    start=True,
+                    stop=True,
+                )
 
         pe_picked = keep.tile([P, S], F32, name="pe_picked")
         nc.vector.tensor_copy(out=pe_picked[:], in_=pe_plane[0][:].indirect(offsets[:]))

@@ -22,7 +22,8 @@ PACK = 4
 HALF_S = S // 2
 CHUNK = 128
 HALF_M = P // 2
-SCALAR_CHANNELS = 40
+LAST = 64
+SCALAR_CHANNELS = 24
 
 
 def tile_picked_posadd_gelu_l_kernel(tc, xT, w1, w2_words, w2_scales, pe, offs, out):
@@ -82,12 +83,12 @@ def tile_picked_posadd_gelu_l_kernel(tc, xT, w1, w2_words, w2_scales, pe, offs, 
 
         for j in range(PACK - 1):
             gather_x(j, 0, S)
-        weave_x(nc.scalar.copy, 0, 0, S)
-        pieces = ((gpsimd_copy, 0, 160), (nc.vector.tensor_copy, 160, HALF_S), (nc.vector.tensor_copy, HALF_S, S))
-        for lo, hi in ((0, 160), (160, 320), (320, S)):
-            gather_x(PACK - 1, lo, hi)
-        for copy, lo, hi in pieces:
-            weave_x(copy, 1, lo, hi)
+        weave_x(gpsimd_copy, 0, 0, CHUNK)
+        weave_x(nc.scalar.copy, 0, CHUNK, S)
+        for lo in range(0, S, CHUNK):
+            gather_x(PACK - 1, lo, lo + CHUNK)
+        for i, copy in enumerate((nc.scalar.copy, gpsimd_copy, nc.vector.tensor_copy, nc.vector.tensor_copy)):
+            weave_x(copy, 1, i * CHUNK, (i + 1) * CHUNK)
 
         x_codes = {}
         x_scales = keep.tile([P, S], U8, name="x_scales", align_bytes=64)
@@ -114,7 +115,7 @@ def tile_picked_posadd_gelu_l_kernel(tc, xT, w1, w2_words, w2_scales, pe, offs, 
             )
         quantize_x(HALF_S, "w1_first")
 
-        w1_codes = keep.tile([P, H], U32, name="w1_codes", align_bytes=64)
+        w1_codes = keep.tile([P, H], U32, name="w1_codes", tag="w1_codes", align_bytes=64)
         w1_scales = keep.tile([P, H], U8, name="w1_scales", align_bytes=64)
         for u in range(2):
             cols = slice(2 * u * P, (2 * u + 2) * P)
@@ -140,71 +141,80 @@ def tile_picked_posadd_gelu_l_kernel(tc, xT, w1, w2_words, w2_scales, pe, offs, 
                 )
 
         pe_picked = keep.tile([P, S], F32, name="pe_picked")
-        nc.vector.tensor_copy(out=pe_picked[:], in_=pe_plane[0][:].indirect(offsets[:]))
-        late = keep.tile([P, 2 * (CHUNK + S)], F32, name="late")
+        late = keep.tile([P, 2, S], F32, name="late")
         summed = keep.tile([P, PACK, S], F32, name="summed")
         product = {
-            (1, 0): summed[:, 0, 0:HALF_S],
-            (1, 1): keep.tile([P, HALF_S], F32, name="product1")[:],
+            1: keep.tile([P, S], F32, name="product1")[:],
+            2: keep.tile([P, S], F32, name="product2")[:],
+            3: late[:, 0, :],
         }
-        for half in range(2):
-            nc.scalar.copy(out=product[1, half], in_=hidden[1][:, half * HALF_S : (half + 1) * HALF_S])
-        whole = {2: keep.tile([P, S], F32, name="product2")[:], 3: late[:, CHUNK : CHUNK + S]}
-        for t in (2, 3):
-            nc.scalar.copy(out=whole[t], in_=hidden[t][:])
-            for half in range(2):
-                product[t, half] = whole[t][:, half * HALF_S : (half + 1) * HALF_S]
+        for t in range(1, PACK):
+            nc.scalar.copy(out=product[t], in_=hidden[t][:])
 
-        late_sums = late[:].rearrange("p (e s) -> p e s", e=2)[:, :, 0:HALF_S]
-        h_grouped = keep.tile([P, S, PACK], BF16, name="h_grouped", align_bytes=64)
+        h_half = [
+            keep.tile([P, HALF_S, PACK], BF16, name="h_half%d" % half, tag=tag, align_bytes=64)
+            for half, tag in enumerate(("x_codes0", "w1_codes"))
+        ]
 
         def gather_add(t, lo, hi, sums):
             nc.vector.tensor_tensor(
                 out=sums,
                 in0=pe_plane[t][:].indirect(offsets[:, lo // 16 : hi // 16]),
-                in1=product[t, lo // HALF_S][:, lo % HALF_S : lo % HALF_S + hi - lo],
+                in1=product[t][:, lo:hi],
                 op=ADD,
             )
 
         def gelu_pair(u, lo, hi, sums):
+            base = lo - lo % HALF_S
             nc.scalar.activation(
-                out=h_grouped[:, lo:hi, 2 * u : 2 * u + 2],
+                out=h_half[lo // HALF_S][:, lo - base : hi - base, 2 * u : 2 * u + 2],
                 in_=sums.rearrange("p e s -> p s e"),
                 func=GELU,
             )
 
         def gelu_quad(lo, hi):
             nc.scalar.activation(
-                out=h_grouped[:, lo:hi, :].rearrange("p (g i) t -> p g t i", i=4),
+                out=h_half[0][:, lo:hi, :].rearrange("p (g i) t -> p g t i", i=4),
                 in_=summed[:, :, lo:hi].rearrange("p t (g i) -> p g t i", i=4),
                 func=GELU,
             )
 
-        for lo in range(0, S, HALF_S):
-            gather_add(1, lo, lo + HALF_S, summed[:, 1, lo : lo + HALF_S])
-        nc.vector.tensor_tensor(out=summed[:, 0, :], in0=hidden[0][:], in1=pe_picked[:], op=ADD)
+        halves = [slice(lo, lo + HALF_S) for lo in range(0, S, HALF_S)]
+        for half in halves:
+            nc.vector.tensor_copy(
+                out=pe_picked[:, half], in_=pe_plane[0][:].indirect(offsets[:, half.start // 16 : half.stop // 16])
+            )
+        for half in halves:
+            nc.vector.tensor_tensor(out=summed[:, 0, half], in0=hidden[0][:, half], in1=pe_picked[:, half], op=ADD)
+        for half in reversed(halves):
+            gather_add(1, half.start, half.stop, summed[:, 1, half])
         gelu_pair(0, HALF_S, S, summed[:, 0:2, HALF_S:S])
+        gelu_pair(0, CHUNK, HALF_S, summed[:, 0:2, CHUNK:HALF_S])
         gather_add(2, 0, HALF_S, summed[:, 2, 0:HALF_S])
         for lo in range(0, HALF_S, CHUNK):
             gather_add(3, lo, lo + CHUNK, summed[:, 3, lo : lo + CHUNK])
-            gelu_quad(lo, lo + CHUNK)
-        gather_add(2, HALF_S, S, late_sums[:, 0, :])
-        for lo in range(0, HALF_S, CHUNK):
-            gather_add(3, HALF_S + lo, HALF_S + lo + CHUNK, late_sums[:, 1, lo : lo + CHUNK])
-            gelu_pair(1, HALF_S + lo, HALF_S + lo + CHUNK, late_sums[:, :, lo : lo + CHUNK])
+        gelu_quad(0, CHUNK)
+        gelu_pair(1, CHUNK, HALF_S, summed[:, 2:4, CHUNK:HALF_S])
+        for lo, cuts in ((0, (0, CHUNK)), (CHUNK, (CHUNK, CHUNK + LAST, HALF_S))):
+            gather_add(2, HALF_S + lo, HALF_S + lo + CHUNK, late[:, 0, lo : lo + CHUNK])
+            for a, b in zip(cuts, cuts[1:]):
+                gather_add(3, HALF_S + a, HALF_S + b, late[:, 1, a:b])
+                gelu_pair(1, HALF_S + a, HALF_S + b, late[:, :, a:b])
 
         h_codes = keep.tile([P, S], U32, name="h_codes", tag="pe_plane2", align_bytes=64)
         h_scales = keep.tile([P, S], U8, name="h_scales", align_bytes=64)
-        for lo, hi, copy in (
-            (0, 256, nc.scalar.copy),
-            (256, 384, nc.scalar.copy),
-            (384, 512, nc.vector.tensor_copy),
+        for cuts, copy in (
+            ((0, 256), nc.scalar.copy),
+            ((256, 384), nc.scalar.copy),
+            ((384, S - LAST, S), nc.vector.tensor_copy),
         ):
-            nc.vector.quantize_mx(
-                out=h_codes[:, lo:hi].bitcast(FP8X4),
-                scales=h_scales[:, lo:hi],
-                in_=h_grouped[:, lo:hi, :].rearrange("p s t -> p (s t)"),
-            )
+            for a, b in zip(cuts, cuts[1:]):
+                nc.vector.quantize_mx(
+                    out=h_codes[:, a:b].bitcast(FP8X4),
+                    scales=h_scales[:, a:b],
+                    in_=h_half[a // HALF_S][:, a % HALF_S : a % HALF_S + b - a, :].rearrange("p s t -> p (s t)"),
+                )
+            lo, hi = cuts[0], cuts[-1]
             acc = psum.tile([P, hi - lo], F32, name="acc%d" % lo)
             nc.tensor.matmul_mx(
                 out=acc[:],

@@ -204,7 +204,8 @@ def tile_picked_posadd_gelu_l_kernel(tc, xT, w1, w2_words, w2_scales, pe, offs, 
         h_codes = keep.tile([P, S], U32, name="h_codes", tag="pe_plane2", align_bytes=64)
         h_scales = keep.tile([P, S], U8, name="h_scales", align_bytes=64)
         for cuts, copy in (
-            ((0, 256), nc.scalar.copy),
+            ((0, 128), nc.scalar.copy),
+            ((128, 256), nc.vector.tensor_copy),
             ((256, 384), nc.scalar.copy),
             ((384, S - LAST, S), nc.vector.tensor_copy),
         ):

@@ -23,7 +23,6 @@ HALF_S = S // 2
 CHUNK = 128
 HALF_M = P // 2
 LAST = 64
-SCALAR_CHANNELS = 24
 
 
 def tile_picked_posadd_gelu_l_kernel(tc, xT, w1, w2_words, w2_scales, pe, offs, out):
@@ -83,11 +82,10 @@ def tile_picked_posadd_gelu_l_kernel(tc, xT, w1, w2_words, w2_scales, pe, offs, 
 
         for j in range(PACK - 1):
             gather_x(j, 0, S)
-        weave_x(gpsimd_copy, 0, 0, CHUNK)
-        weave_x(nc.scalar.copy, 0, CHUNK, S)
+        weave_x(nc.scalar.copy, 0, 0, S)
         for lo in range(0, S, CHUNK):
             gather_x(PACK - 1, lo, lo + CHUNK)
-        for i, copy in enumerate((nc.scalar.copy, gpsimd_copy, nc.vector.tensor_copy, nc.vector.tensor_copy)):
+        for i, copy in enumerate((gpsimd_copy, gpsimd_copy, nc.vector.tensor_copy, nc.vector.tensor_copy)):
             weave_x(copy, 1, i * CHUNK, (i + 1) * CHUNK)
 
         x_codes = {}
@@ -105,13 +103,13 @@ def tile_picked_posadd_gelu_l_kernel(tc, xT, w1, w2_words, w2_scales, pe, offs, 
 
         w1_grouped = keep.tile([P, PACK, P, PACK], BF16, name="w1_grouped", align_bytes=64)
         for copy, half, lo, hi in (
-            (nc.scalar.copy, 0, 0, HALF_M),
-            (nc.scalar.copy, 1, 0, SCALAR_CHANNELS),
-            (nc.vector.tensor_copy, 1, SCALAR_CHANNELS, HALF_M),
+            (nc.scalar.copy, 0, 0, PACK),
+            (nc.vector.tensor_copy, 1, 0, 2),
+            (nc.scalar.copy, 1, 2, PACK),
         ):
             copy(
-                out=w1_grouped[:, :, half * HALF_M + lo : half * HALF_M + hi, :].rearrange("p t m j -> p m j t"),
-                in_=w1_raw[half][:, :, PACK * lo : PACK * hi].rearrange("p j (m t) -> p m j t", t=PACK),
+                out=w1_grouped[:, lo:hi, half * HALF_M : (half + 1) * HALF_M, :].rearrange("p t m j -> p m j t"),
+                in_=w1_raw[half][:].rearrange("p j (m t) -> p m j t", t=PACK)[:, :, :, lo:hi],
             )
         quantize_x(HALF_S, "w1_first")
 

@@ -80,12 +80,20 @@ def tile_picked_posadd_gelu_l_kernel(tc, xT, w1, w2_words, w2_scales, pe, offs, 
                 in_=x_found[:, 2 * u : 2 * u + 2, lo:hi].rearrange("p e s -> p s e"),
             )
 
-        for j in range(PACK - 1):
+        def gather_x_in_place(j, lo, hi):
+            nc.vector.tensor_copy(
+                out=x_picked[:, lo:hi, j], in_=x_plane[j][:].indirect(offsets[:, lo // 16 : hi // 16])
+            )
+
+        for j in range(2):
             gather_x(j, 0, S)
         weave_x(nc.scalar.copy, 0, 0, S)
-        for lo in range(0, S, CHUNK):
-            gather_x(PACK - 1, lo, lo + CHUNK)
-        for i, copy in enumerate((gpsimd_copy, gpsimd_copy, nc.vector.tensor_copy, nc.vector.tensor_copy)):
+        gather_x(2, 0, S - CHUNK)
+        gather_x_in_place(2, S - CHUNK, S)
+        gather_x(3, 0, CHUNK)
+        gather_x(3, CHUNK, S - CHUNK)
+        gather_x_in_place(3, S - CHUNK, S)
+        for i, copy in enumerate((gpsimd_copy, nc.vector.tensor_copy, nc.vector.tensor_copy)):
             weave_x(copy, 1, i * CHUNK, (i + 1) * CHUNK)
 
         x_codes = {}
@@ -115,39 +123,51 @@ def tile_picked_posadd_gelu_l_kernel(tc, xT, w1, w2_words, w2_scales, pe, offs, 
 
         w1_codes = keep.tile([P, H], U32, name="w1_codes", tag="w1_codes", align_bytes=64)
         w1_scales = keep.tile([P, H], U8, name="w1_scales", align_bytes=64)
-        for u in range(2):
-            cols = slice(2 * u * P, (2 * u + 2) * P)
+        for lo, hi in ((0, 1), (1, 2), (2, 4)):
+            cols = slice(lo * P, hi * P)
             nc.vector.quantize_mx(
                 out=w1_codes[:, cols].bitcast(FP8X4),
                 scales=w1_scales[:, cols],
-                in_=w1_grouped[:, 2 * u : 2 * u + 2, :, :].rearrange("p t m j -> p (t m j)"),
+                in_=w1_grouped[:, lo:hi, :, :].rearrange("p t m j -> p (t m j)"),
             )
 
-        hidden = {}
-        for t in (1, 0, 2, 3):
-            hidden[t] = psum.tile([P, S], F32, name="hidden%d" % t)
-            rows = slice(t * P, (t + 1) * P)
-            for lo in range(0, S, HALF_S):
-                nc.tensor.matmul_mx(
-                    out=hidden[t][:, lo : lo + HALF_S],
-                    lhsT=w1_codes[:, rows].bitcast(FP8X4),
-                    lhsT_scale=w1_scales[:, rows],
-                    rhs=x_codes[lo][:].bitcast(FP8X4),
-                    rhs_scale=x_scales[:, lo : lo + HALF_S],
-                    start=True,
-                    stop=True,
-                )
-
-        pe_picked = keep.tile([P, S], F32, name="pe_picked")
+        pe_picked = keep.tile([P, HALF_S], F32, name="pe_picked")
         late = keep.tile([P, 2, S], F32, name="late")
         summed = keep.tile([P, PACK, S], F32, name="summed")
         product = {
+            0: keep.tile([P, HALF_S], F32, name="product0")[:],
             1: keep.tile([P, S], F32, name="product1")[:],
             2: keep.tile([P, S], F32, name="product2")[:],
             3: late[:, 0, :],
         }
-        for t in range(1, PACK):
-            nc.scalar.copy(out=product[t], in_=hidden[t][:])
+        banks = (
+            (0, 0, CHUNK),
+            (0, CHUNK, HALF_S),
+            (1, HALF_S, S),
+            (0, HALF_S, S),
+            (1, 0, HALF_S),
+            (2, 0, S),
+            (3, 0, S),
+        )
+        for i, (t, first, last) in enumerate(banks):
+            hidden = psum.tile([P, last - first], F32, name="hidden%d" % i, tag="bank%d" % i)
+            rows = slice(t * P, (t + 1) * P)
+            for lo in range(first, last, HALF_S):
+                hi = min(lo + HALF_S, last)
+                base = lo - lo % HALF_S
+                nc.tensor.matmul_mx(
+                    out=hidden[:, lo - first : hi - first],
+                    lhsT=w1_codes[:, rows].bitcast(FP8X4),
+                    lhsT_scale=w1_scales[:, rows],
+                    rhs=x_codes[base][:, lo - base : hi - base].bitcast(FP8X4),
+                    rhs_scale=x_scales[:, lo:hi],
+                    start=True,
+                    stop=True,
+                )
+            if (t, first) == (0, HALF_S):
+                kept_in_psum = hidden
+            else:
+                nc.scalar.copy(out=product[t][:, first:last], in_=hidden[:])
 
         h_half = [
             keep.tile([P, HALF_S, PACK], BF16, name="h_half%d" % half, tag=tag, align_bytes=64)
@@ -178,12 +198,10 @@ def tile_picked_posadd_gelu_l_kernel(tc, xT, w1, w2_words, w2_scales, pe, offs, 
             )
 
         halves = [slice(lo, lo + HALF_S) for lo in range(0, S, HALF_S)]
-        for half in halves:
-            nc.vector.tensor_copy(
-                out=pe_picked[:, half], in_=pe_plane[0][:].indirect(offsets[:, half.start // 16 : half.stop // 16])
-            )
-        for half in halves:
-            nc.vector.tensor_tensor(out=summed[:, 0, half], in0=hidden[0][:, half], in1=pe_picked[:, half], op=ADD)
+        nc.vector.tensor_copy(out=pe_picked[:], in_=pe_plane[0][:].indirect(offsets[:, HALF_S // 16 : S // 16]))
+        for lo in range(0, HALF_S, CHUNK):
+            gather_add(0, lo, lo + CHUNK, summed[:, 0, lo : lo + CHUNK])
+        nc.vector.tensor_tensor(out=summed[:, 0, HALF_S:S], in0=kept_in_psum[:], in1=pe_picked[:], op=ADD)
         for half in reversed(halves):
             gather_add(1, half.start, half.stop, summed[:, 1, half])
         gelu_pair(0, HALF_S, S, summed[:, 0:2, HALF_S:S])
@@ -214,7 +232,7 @@ def tile_picked_posadd_gelu_l_kernel(tc, xT, w1, w2_words, w2_scales, pe, offs, 
                     in_=h_half[a // HALF_S][:, a % HALF_S : a % HALF_S + b - a, :].rearrange("p s t -> p (s t)"),
                 )
             lo, hi = cuts[0], cuts[-1]
-            acc = psum.tile([P, hi - lo], F32, name="acc%d" % lo)
+            acc = psum.tile([P, hi - lo], F32, name="acc%d" % lo, tag="bank%d" % ((lo // CHUNK + 7) % 8))
             nc.tensor.matmul_mx(
                 out=acc[:],
                 lhsT=w2_codes[:].bitcast(FP4X4),

@@ -144,13 +144,15 @@ def tile_picked_posadd_gelu_l_kernel(tc, xT, w1, w2_words, w2_scales, pe, offs, 
             (0, 0, CHUNK),
             (0, CHUNK, HALF_S),
             (1, HALF_S, S),
-            (0, HALF_S, S),
             (1, 0, HALF_S),
-            (2, 0, S),
-            (3, 0, S),
+            (2, 0, HALF_S),
+            (0, HALF_S, S),
+            (2, HALF_S, S),
+            (3, 0, HALF_S),
+            (3, HALF_S, S),
         )
         for i, (t, first, last) in enumerate(banks):
-            hidden = psum.tile([P, last - first], F32, name="hidden%d" % i, tag="bank%d" % i)
+            hidden = psum.tile([P, last - first], F32, name="hidden%d" % i, tag="bank%d" % (i % 8))
             rows = slice(t * P, (t + 1) * P)
             for lo in range(first, last, HALF_S):
                 hi = min(lo + HALF_S, last)
@@ -197,13 +199,12 @@ def tile_picked_posadd_gelu_l_kernel(tc, xT, w1, w2_words, w2_scales, pe, offs, 
                 func=GELU,
             )
 
-        halves = [slice(lo, lo + HALF_S) for lo in range(0, S, HALF_S)]
         nc.vector.tensor_copy(out=pe_picked[:], in_=pe_plane[0][:].indirect(offsets[:, HALF_S // 16 : S // 16]))
         for lo in range(0, HALF_S, CHUNK):
             gather_add(0, lo, lo + CHUNK, summed[:, 0, lo : lo + CHUNK])
+        gather_add(1, HALF_S, S, summed[:, 1, HALF_S:S])
         nc.vector.tensor_tensor(out=summed[:, 0, HALF_S:S], in0=kept_in_psum[:], in1=pe_picked[:], op=ADD)
-        for half in reversed(halves):
-            gather_add(1, half.start, half.stop, summed[:, 1, half])
+        gather_add(1, 0, HALF_S, summed[:, 1, 0:HALF_S])
         gelu_pair(0, HALF_S, S, summed[:, 0:2, HALF_S:S])
         gelu_pair(0, CHUNK, HALF_S, summed[:, 0:2, CHUNK:HALF_S])
         gather_add(2, 0, HALF_S, summed[:, 2, 0:HALF_S])
@@ -232,7 +233,7 @@ def tile_picked_posadd_gelu_l_kernel(tc, xT, w1, w2_words, w2_scales, pe, offs, 
                     in_=h_half[a // HALF_S][:, a % HALF_S : a % HALF_S + b - a, :].rearrange("p s t -> p (s t)"),
                 )
             lo, hi = cuts[0], cuts[-1]
-            acc = psum.tile([P, hi - lo], F32, name="acc%d" % lo, tag="bank%d" % ((lo // CHUNK + 7) % 8))
+            acc = psum.tile([P, hi - lo], F32, name="acc%d" % lo, tag="bank%d" % (lo // CHUNK + 1))
             nc.tensor.matmul_mx(
                 out=acc[:],
                 lhsT=w2_codes[:].bitcast(FP4X4),

@@ -14,6 +14,7 @@ U8 = mybir.dt.uint8
 FP8X4 = mybir.dt.float8_e4m3fn_x4
 FP4X4 = mybir.dt.float4_e2m1fn_x4
 GELU = mybir.ActivationFunctionType.Gelu_apprx_tanh
+COPY = mybir.ActivationFunctionType.Copy
 MULT = mybir.AluOpType.mult
 ADD = mybir.AluOpType.add
 
@@ -66,10 +67,12 @@ def tile_picked_posadd_gelu_l_kernel(tc, xT, w1, w2_words, w2_scales, pe, offs, 
             )
 
         x_picked = keep.tile([P, S, PACK], BF16, name="x_picked", align_bytes=64)
-        x_found = keep.tile([P, PACK, S], F32, name="x_found")
+        x_found = [keep.tile([P, 2, S], dtype, name="x_found%d" % u) for u, dtype in enumerate((BF16, F32))]
 
         def gather_x(j, lo, hi):
-            nc.vector.tensor_copy(out=x_found[:, j, lo:hi], in_=x_plane[j][:].indirect(offsets[:, lo // 16 : hi // 16]))
+            nc.vector.tensor_copy(
+                out=x_found[1][:, j - 2, lo:hi], in_=x_plane[j][:].indirect(offsets[:, lo // 16 : hi // 16])
+            )
 
         def gpsimd_copy(out, in_):
             nc.gpsimd.tensor_scalar(out, in_, 1.0, 0.0, MULT, ADD)
@@ -77,7 +80,7 @@ def tile_picked_posadd_gelu_l_kernel(tc, xT, w1, w2_words, w2_scales, pe, offs, 
         def weave_x(copy, u, lo, hi):
             copy(
                 out=x_picked[:, lo:hi, 2 * u : 2 * u + 2],
-                in_=x_found[:, 2 * u : 2 * u + 2, lo:hi].rearrange("p e s -> p s e"),
+                in_=x_found[u][:, :, lo:hi].rearrange("p e s -> p s e"),
             )
 
         def gather_x_in_place(j, lo, hi):
@@ -85,9 +88,16 @@ def tile_picked_posadd_gelu_l_kernel(tc, xT, w1, w2_words, w2_scales, pe, offs, 
                 out=x_picked[:, lo:hi, j], in_=x_plane[j][:].indirect(offsets[:, lo // 16 : hi // 16])
             )
 
-        for j in range(2):
-            gather_x(j, 0, S)
-        weave_x(nc.scalar.copy, 0, 0, S)
+        for j, cuts in enumerate(((0, S), (CHUNK, S))):
+            x_rounded = keep.tile([P, T], BF16, name="x_rounded%d" % j)
+            nc.vector.tensor_copy(out=x_rounded[:], in_=x_plane[j][:])
+            for lo, hi in zip(cuts, cuts[1:]):
+                nc.scalar.activation(
+                    out=x_found[0][:, j, lo:hi], in_=x_rounded[:].indirect(offsets[:, lo // 16 : hi // 16]), func=COPY
+                )
+        nc.vector.tensor_copy(out=x_found[0][:, 1, 0:CHUNK], in_=x_plane[1][:].indirect(offsets[:, 0 : CHUNK // 16]))
+        weave_x(gpsimd_copy, 0, 0, CHUNK)
+        weave_x(nc.scalar.copy, 0, CHUNK, S)
         gather_x(2, 0, S - CHUNK)
         gather_x_in_place(2, S - CHUNK, S)
         gather_x(3, 0, CHUNK)

@@ -42,10 +42,11 @@ def tile_picked_posadd_gelu_l_kernel(tc, xT, w1, w2_words, w2_scales, pe, offs, 
         pe_rows = pe.rearrange("(p j) c -> p j c", j=PACK)
 
         offsets = keep.tile([P, S // 16], U16, name="offsets")
-        nc.sync.dma_start(offsets[:], offs)
         x_plane = [keep.tile([P, T], F32, name="x_plane%d" % j) for j in range(PACK)]
         for j in range(PACK):
             nc.sync.dma_start(out=x_plane[j][:], in_=x_rows[:, j, :])
+            if j == 0:
+                nc.sync.dma_start(offsets[:], offs)
         pe_plane = [keep.tile([P, T], F32, name="pe_plane%d" % t, align_bytes=64) for t in range(PACK)]
         w1_raw = [
             keep.tile([P, PACK, H // 2], F32, name="w1_raw%d" % half, tag=tag, align_bytes=64)

@@ -231,6 +231,8 @@ def tile_picked_posadd_gelu_l_kernel(tc, xT, w1, w2_words, w2_scales, pe, offs, 
 
         h_codes = keep.tile([P, S], U32, name="h_codes", tag="pe_plane2", align_bytes=64)
         h_scales = keep.tile([P, S], U8, name="h_scales", align_bytes=64)
+        result = keep.tile([P, S], F32, name="result")
+        store_from = {CHUNK: 0, S - CHUNK: CHUNK, S: S - CHUNK}
         for cuts, copy in (
             ((0, 128), nc.scalar.copy),
             ((128, 256), nc.vector.tensor_copy),
@@ -254,6 +256,6 @@ def tile_picked_posadd_gelu_l_kernel(tc, xT, w1, w2_words, w2_scales, pe, offs, 
                 start=True,
                 stop=True,
             )
-            result = keep.tile([P, hi - lo], F32, name="result%d" % lo)
-            copy(out=result[:], in_=acc[:])
-            nc.sync.dma_start(out=out[:, lo:hi], in_=result[:])
+            copy(out=result[:, lo:hi], in_=acc[:])
+            if hi in store_from:
+                nc.sync.dma_start(out=out[:, store_from[hi] : hi], in_=result[:, store_from[hi] : hi])

@@ -151,6 +151,9 @@ def tile_picked_posadd_gelu_l_kernel(tc, xT, w1, w2_words, w2_scales, pe, offs, 
             2: keep.tile([P, S], F32, name="product2")[:],
             3: late[:, 0, :],
         }
+        nc.scalar.activation(
+            out=pe_picked[:, HALF_S - LAST :], in_=pe_plane[0][:].indirect(offsets[:, (S - LAST) // 16 :]), func=COPY
+        )
         banks = (
             (0, 0, CHUNK),
             (0, CHUNK, HALF_S),
@@ -210,7 +213,9 @@ def tile_picked_posadd_gelu_l_kernel(tc, xT, w1, w2_words, w2_scales, pe, offs, 
                 func=GELU,
             )
 
-        nc.vector.tensor_copy(out=pe_picked[:], in_=pe_plane[0][:].indirect(offsets[:, HALF_S // 16 : S // 16]))
+        nc.vector.tensor_copy(
+            out=pe_picked[:, 0 : HALF_S - LAST], in_=pe_plane[0][:].indirect(offsets[:, HALF_S // 16 : (S - LAST) // 16])
+        )
         for lo in range(0, HALF_S, CHUNK):
             gather_add(0, lo, lo + CHUNK, summed[:, 0, lo : lo + CHUNK])
         gather_add(1, HALF_S, S, summed[:, 1, HALF_S:S])
@@ -231,8 +236,6 @@ def tile_picked_posadd_gelu_l_kernel(tc, xT, w1, w2_words, w2_scales, pe, offs, 
 
         h_codes = keep.tile([P, S], U32, name="h_codes", tag="pe_plane2", align_bytes=64)
         h_scales = keep.tile([P, S], U8, name="h_scales", align_bytes=64)
-        result = keep.tile([P, S], F32, name="result")
-        store_from = {CHUNK: 0, S - CHUNK: CHUNK, S: S - CHUNK}
         for cuts, copy in (
             ((0, 128), nc.scalar.copy),
             ((128, 256), nc.vector.tensor_copy),
@@ -256,6 +259,6 @@ def tile_picked_posadd_gelu_l_kernel(tc, xT, w1, w2_words, w2_scales, pe, offs, 
                 start=True,
                 stop=True,
             )
-            copy(out=result[:, lo:hi], in_=acc[:])
-            if hi in store_from:
-                nc.sync.dma_start(out=out[:, store_from[hi] : hi], in_=result[:, store_from[hi] : hi])
+            result = keep.tile([P, hi - lo], F32, name="result%d" % lo)
+            copy(out=result[:], in_=acc[:])
+            nc.sync.dma_start(out=out[:, lo:hi], in_=result[:])

@@ -15,15 +15,14 @@ FP8X4 = mybir.dt.float8_e4m3fn_x4
 FP4X4 = mybir.dt.float4_e2m1fn_x4
 GELU = mybir.ActivationFunctionType.Gelu_apprx_tanh
 COPY = mybir.ActivationFunctionType.Copy
-MULT = mybir.AluOpType.mult
 ADD = mybir.AluOpType.add
 
 P = 128
 PACK = 4
 HALF_S = S // 2
 CHUNK = 128
-HALF_M = P // 2
 LAST = 64
+X_VECTOR = 288
 
 
 def tile_picked_posadd_gelu_l_kernel(tc, xT, w1, w2_words, w2_scales, pe, offs, out):
@@ -47,90 +46,54 @@ def tile_picked_posadd_gelu_l_kernel(tc, xT, w1, w2_words, w2_scales, pe, offs, 
             nc.sync.dma_start(out=x_plane[j][:], in_=x_rows[:, j, :])
             if j == 0:
                 nc.sync.dma_start(offsets[:], offs)
+        w1_raw = [keep.tile([P, 2, H], F32, name="w1_raw%d" % u) for u in range(2)]
+        for u in range(2):
+            nc.sync.dma_start(out=w1_raw[u][:], in_=w1_rows[:, 2 * u : 2 * u + 2, :])
         pe_plane = [keep.tile([P, T], F32, name="pe_plane%d" % t, align_bytes=64) for t in range(PACK)]
-        w1_raw = [
-            keep.tile([P, PACK, H // 2], F32, name="w1_raw%d" % half, tag=tag, align_bytes=64)
-            for half, tag in enumerate(("w1_first", "w1_second"))
-        ]
-        for half in range(2):
-            nc.sync.dma_start(out=w1_raw[half][:], in_=w1_rows[:, :, half * (H // 2) : (half + 1) * (H // 2)])
         for t in range(PACK):
             nc.sync.dma_start(out=pe_plane[t][:], in_=pe_rows[:, t, :])
 
         w2_codes = keep.tile([P, 2 * N], U8, name="w2_codes", align_bytes=64)
         nc.sync.dma_start(out=w2_codes[:].bitcast(I32), in_=w2_words[0].bitcast(I32))
         w2_plane = keep.tile([P, N], U8, name="w2_plane", align_bytes=64)
-        nc.gpsimd.memset(w2_plane[:].bitcast(I32), 0)
+        nc.vector.memset(w2_plane[:].bitcast(I32), 0)
         for q in range(4):
             nc.sync.dma_start(
                 out=w2_plane[32 * q : 32 * q + 4, :].bitcast(I32),
                 in_=w2_scales[0, 4 * q : 4 * q + 4, :].bitcast(I32),
             )
 
+        def picked(plane, lo, hi):
+            return plane[:].indirect(offsets[:, lo // 16 : hi // 16])
+
         x_picked = keep.tile([P, S, PACK], BF16, name="x_picked", align_bytes=64)
-        x_found = [keep.tile([P, 2, S], dtype, name="x_found%d" % u) for u, dtype in enumerate((BF16, F32))]
-
-        def gather_x(j, lo, hi):
-            nc.vector.tensor_copy(
-                out=x_found[1][:, j - 2, lo:hi], in_=x_plane[j][:].indirect(offsets[:, lo // 16 : hi // 16])
-            )
-
-        def gpsimd_copy(out, in_):
-            nc.gpsimd.tensor_scalar(out, in_, 1.0, 0.0, MULT, ADD)
-
-        def weave_x(copy, u, lo, hi):
-            copy(
-                out=x_picked[:, lo:hi, 2 * u : 2 * u + 2],
-                in_=x_found[u][:, :, lo:hi].rearrange("p e s -> p s e"),
-            )
-
-        def gather_x_in_place(j, lo, hi):
-            nc.vector.tensor_copy(
-                out=x_picked[:, lo:hi, j], in_=x_plane[j][:].indirect(offsets[:, lo // 16 : hi // 16])
-            )
-
-        for j, cuts in enumerate(((0, S), (CHUNK, S))):
-            x_rounded = keep.tile([P, T], BF16, name="x_rounded%d" % j)
-            nc.vector.tensor_copy(out=x_rounded[:], in_=x_plane[j][:])
+        for j in range(PACK):
+            cuts = (0, CHUNK, X_VECTOR) if j == PACK - 1 else (0, X_VECTOR)
             for lo, hi in zip(cuts, cuts[1:]):
-                nc.scalar.activation(
-                    out=x_found[0][:, j, lo:hi], in_=x_rounded[:].indirect(offsets[:, lo // 16 : hi // 16]), func=COPY
-                )
-        nc.vector.tensor_copy(out=x_found[0][:, 1, 0:CHUNK], in_=x_plane[1][:].indirect(offsets[:, 0 : CHUNK // 16]))
-        weave_x(gpsimd_copy, 0, 0, CHUNK)
-        weave_x(nc.scalar.copy, 0, CHUNK, S)
-        gather_x(2, 0, S - CHUNK)
-        gather_x_in_place(2, S - CHUNK, S)
-        gather_x(3, 0, CHUNK)
-        gather_x(3, CHUNK, S - CHUNK)
-        gather_x_in_place(3, S - CHUNK, S)
-        for i, copy in enumerate((gpsimd_copy, nc.vector.tensor_copy, nc.vector.tensor_copy)):
-            weave_x(copy, 1, i * CHUNK, (i + 1) * CHUNK)
+                nc.vector.tensor_copy(out=x_picked[:, lo:hi, j], in_=picked(x_plane[j], lo, hi))
+            nc.scalar.activation(out=x_picked[:, X_VECTOR:S, j], in_=picked(x_plane[j], X_VECTOR, S), func=COPY)
 
-        x_codes = {}
+        x_codes = keep.tile([P, S], U32, name="x_codes", align_bytes=64)
         x_scales = keep.tile([P, S], U8, name="x_scales", align_bytes=64)
-
-        def quantize_x(lo, tag):
-            x_codes[lo] = keep.tile([P, HALF_S], U32, name="x_codes%d" % lo, tag=tag, align_bytes=64)
+        for lo, hi in ((0, CHUNK), (CHUNK, S)):
             nc.vector.quantize_mx(
-                out=x_codes[lo][:].bitcast(FP8X4),
-                scales=x_scales[:, lo : lo + HALF_S],
-                in_=x_picked[:, lo : lo + HALF_S, :].rearrange("p s j -> p (s j)"),
+                out=x_codes[:, lo:hi].bitcast(FP8X4),
+                scales=x_scales[:, lo:hi],
+                in_=x_picked[:, lo:hi, :].rearrange("p s j -> p (s j)"),
             )
-
-        quantize_x(0, "x_codes0")
 
         w1_grouped = keep.tile([P, PACK, P, PACK], BF16, name="w1_grouped", align_bytes=64)
-        for copy, half, lo, hi in (
-            (nc.scalar.copy, 0, 0, PACK),
-            (nc.vector.tensor_copy, 1, 0, 2),
+        for copy, u, lo, hi in (
+            (nc.vector.tensor_copy, 0, 0, 2),
+            (nc.scalar.copy, 0, 2, PACK),
+            (nc.vector.tensor_copy, 1, 0, 1),
+            (nc.vector.tensor_copy, 1, 1, 2),
             (nc.scalar.copy, 1, 2, PACK),
         ):
             copy(
-                out=w1_grouped[:, lo:hi, half * HALF_M : (half + 1) * HALF_M, :].rearrange("p t m j -> p m j t"),
-                in_=w1_raw[half][:].rearrange("p j (m t) -> p m j t", t=PACK)[:, :, :, lo:hi],
+                out=w1_grouped[:, lo:hi, :, 2 * u : 2 * u + 2].rearrange("p t m e -> p m e t"),
+                in_=w1_raw[u][:].rearrange("p e (m t) -> p m e t", t=PACK)[:, :, :, lo:hi],
             )
-        quantize_x(HALF_S, "w1_first")
 
         w1_codes = keep.tile([P, H], U32, name="w1_codes", tag="w1_codes", align_bytes=64)
         w1_scales = keep.tile([P, H], U8, name="w1_scales", align_bytes=64)
@@ -168,18 +131,15 @@ def tile_picked_posadd_gelu_l_kernel(tc, xT, w1, w2_words, w2_scales, pe, offs, 
         for i, (t, first, last) in enumerate(banks):
             hidden = psum.tile([P, last - first], F32, name="hidden%d" % i, tag="bank%d" % (i % 8))
             rows = slice(t * P, (t + 1) * P)
-            for lo in range(first, last, HALF_S):
-                hi = min(lo + HALF_S, last)
-                base = lo - lo % HALF_S
-                nc.tensor.matmul_mx(
-                    out=hidden[:, lo - first : hi - first],
-                    lhsT=w1_codes[:, rows].bitcast(FP8X4),
-                    lhsT_scale=w1_scales[:, rows],
-                    rhs=x_codes[base][:, lo - base : hi - base].bitcast(FP8X4),
-                    rhs_scale=x_scales[:, lo:hi],
-                    start=True,
-                    stop=True,
-                )
+            nc.tensor.matmul_mx(
+                out=hidden[:],
+                lhsT=w1_codes[:, rows].bitcast(FP8X4),
+                lhsT_scale=w1_scales[:, rows],
+                rhs=x_codes[:, first:last].bitcast(FP8X4),
+                rhs_scale=x_scales[:, first:last],
+                start=True,
+                stop=True,
+            )
             if (t, first) == (0, HALF_S):
                 kept_in_psum = hidden
             else:
@@ -187,7 +147,7 @@ def tile_picked_posadd_gelu_l_kernel(tc, xT, w1, w2_words, w2_scales, pe, offs, 
 
         h_half = [
             keep.tile([P, HALF_S, PACK], BF16, name="h_half%d" % half, tag=tag, align_bytes=64)
-            for half, tag in enumerate(("x_codes0", "w1_codes"))
+            for half, tag in enumerate(("x_codes", "w1_codes"))
         ]
 
         def gather_add(t, lo, hi, sums):

from contextlib import ExitStack

import concourse.mybir as mybir

K, T, S, H, N = 512, 1024, 512, 512, 128
FLOPS = 2 * K * H * S + 2 * H * N * S

F32 = mybir.dt.float32
BF16 = mybir.dt.bfloat16
I32 = mybir.dt.int32
U32 = mybir.dt.uint32
U16 = mybir.dt.uint16
U8 = mybir.dt.uint8
FP8X4 = mybir.dt.float8_e4m3fn_x4
FP4X4 = mybir.dt.float4_e2m1fn_x4
GELU = mybir.ActivationFunctionType.Gelu_apprx_tanh
COPY = mybir.ActivationFunctionType.Copy
ADD = mybir.AluOpType.add

P = 128
PACK = 4
HALF_S = S // 2
CHUNK = 128
LAST = 64
X_VECTOR = 288


def tile_picked_posadd_gelu_l_kernel(tc, xT, w1, w2_words, w2_scales, pe, offs, out):
    nc = tc.nc
    with ExitStack() as ctx:
        keep = ctx.enter_context(tc.tile_pool(name="keep", bufs=1))
        psum = ctx.enter_context(tc.psum_pool(name="psum", bufs=1))

        warm_in = keep.tile([P, 1], F32, name="warm_in")
        warm_out = keep.tile([P, 1], F32, name="warm_out")
        nc.vector.memset(warm_in[:], 0.0)
        nc.scalar.activation(out=warm_out[:], in_=warm_in[:], func=GELU)

        x_rows = xT.rearrange("(p j) c -> p j c", j=PACK)
        w1_rows = w1.rearrange("(p j) c -> p j c", j=PACK)
        pe_rows = pe.rearrange("(p j) c -> p j c", j=PACK)

        offsets = keep.tile([P, S // 16], U16, name="offsets")
        x_plane = [keep.tile([P, T], F32, name="x_plane%d" % j) for j in range(PACK)]
        for j in range(PACK):
            nc.sync.dma_start(out=x_plane[j][:], in_=x_rows[:, j, :])
            if j == 0:
                nc.sync.dma_start(offsets[:], offs)
        w1_raw = [keep.tile([P, 2, H], F32, name="w1_raw%d" % u) for u in range(2)]
        for u in range(2):
            nc.sync.dma_start(out=w1_raw[u][:], in_=w1_rows[:, 2 * u : 2 * u + 2, :])
        pe_plane = [keep.tile([P, T], F32, name="pe_plane%d" % t, align_bytes=64) for t in range(PACK)]
        for t in range(PACK):
            nc.sync.dma_start(out=pe_plane[t][:], in_=pe_rows[:, t, :])

        w2_codes = keep.tile([P, 2 * N], U8, name="w2_codes", align_bytes=64)
        nc.sync.dma_start(out=w2_codes[:].bitcast(I32), in_=w2_words[0].bitcast(I32))
        w2_plane = keep.tile([P, N], U8, name="w2_plane", align_bytes=64)
        nc.vector.memset(w2_plane[:].bitcast(I32), 0)
        for q in range(4):
            nc.sync.dma_start(
                out=w2_plane[32 * q : 32 * q + 4, :].bitcast(I32),
                in_=w2_scales[0, 4 * q : 4 * q + 4, :].bitcast(I32),
            )

        def picked(plane, lo, hi):
            return plane[:].indirect(offsets[:, lo // 16 : hi // 16])

        x_picked = keep.tile([P, S, PACK], BF16, name="x_picked", align_bytes=64)
        for j in range(PACK):
            cuts = (0, CHUNK, X_VECTOR) if j == PACK - 1 else (0, X_VECTOR)
            for lo, hi in zip(cuts, cuts[1:]):
                nc.vector.tensor_copy(out=x_picked[:, lo:hi, j], in_=picked(x_plane[j], lo, hi))
            nc.scalar.activation(out=x_picked[:, X_VECTOR:S, j], in_=picked(x_plane[j], X_VECTOR, S), func=COPY)

        x_codes = keep.tile([P, S], U32, name="x_codes", align_bytes=64)
        x_scales = keep.tile([P, S], U8, name="x_scales", align_bytes=64)
        for lo, hi in ((0, CHUNK), (CHUNK, S)):
            nc.vector.quantize_mx(
                out=x_codes[:, lo:hi].bitcast(FP8X4),
                scales=x_scales[:, lo:hi],
                in_=x_picked[:, lo:hi, :].rearrange("p s j -> p (s j)"),
            )

        w1_grouped = keep.tile([P, PACK, P, PACK], BF16, name="w1_grouped", align_bytes=64)
        for copy, u, lo, hi in (
            (nc.vector.tensor_copy, 0, 0, 2),
            (nc.scalar.copy, 0, 2, PACK),
            (nc.vector.tensor_copy, 1, 0, 1),
            (nc.vector.tensor_copy, 1, 1, 2),
            (nc.scalar.copy, 1, 2, PACK),
        ):
            copy(
                out=w1_grouped[:, lo:hi, :, 2 * u : 2 * u + 2].rearrange("p t m e -> p m e t"),
                in_=w1_raw[u][:].rearrange("p e (m t) -> p m e t", t=PACK)[:, :, :, lo:hi],
            )

        w1_codes = keep.tile([P, H], U32, name="w1_codes", tag="w1_codes", align_bytes=64)
        w1_scales = keep.tile([P, H], U8, name="w1_scales", align_bytes=64)
        for lo, hi in ((0, 1), (1, 2), (2, 4)):
            cols = slice(lo * P, hi * P)
            nc.vector.quantize_mx(
                out=w1_codes[:, cols].bitcast(FP8X4),
                scales=w1_scales[:, cols],
                in_=w1_grouped[:, lo:hi, :, :].rearrange("p t m j -> p (t m j)"),
            )

        pe_picked = keep.tile([P, HALF_S], F32, name="pe_picked")
        late = keep.tile([P, 2, S], F32, name="late")
        summed = keep.tile([P, PACK, S], F32, name="summed")
        product = {
            0: keep.tile([P, HALF_S], F32, name="product0")[:],
            1: keep.tile([P, S], F32, name="product1")[:],
            2: keep.tile([P, S], F32, name="product2")[:],
            3: late[:, 0, :],
        }
        nc.scalar.activation(
            out=pe_picked[:, HALF_S - LAST :], in_=pe_plane[0][:].indirect(offsets[:, (S - LAST) // 16 :]), func=COPY
        )
        banks = (
            (0, 0, CHUNK),
            (0, CHUNK, HALF_S),
            (1, HALF_S, S),
            (1, 0, HALF_S),
            (2, 0, HALF_S),
            (0, HALF_S, S),
            (2, HALF_S, S),
            (3, 0, HALF_S),
            (3, HALF_S, S),
        )
        for i, (t, first, last) in enumerate(banks):
            hidden = psum.tile([P, last - first], F32, name="hidden%d" % i, tag="bank%d" % (i % 8))
            rows = slice(t * P, (t + 1) * P)
            nc.tensor.matmul_mx(
                out=hidden[:],
                lhsT=w1_codes[:, rows].bitcast(FP8X4),
                lhsT_scale=w1_scales[:, rows],
                rhs=x_codes[:, first:last].bitcast(FP8X4),
                rhs_scale=x_scales[:, first:last],
                start=True,
                stop=True,
            )
            if (t, first) == (0, HALF_S):
                kept_in_psum = hidden
            else:
                nc.scalar.copy(out=product[t][:, first:last], in_=hidden[:])

        h_half = [
            keep.tile([P, HALF_S, PACK], BF16, name="h_half%d" % half, tag=tag, align_bytes=64)
            for half, tag in enumerate(("x_codes", "w1_codes"))
        ]

        def gather_add(t, lo, hi, sums):
            nc.vector.tensor_tensor(
                out=sums,
                in0=pe_plane[t][:].indirect(offsets[:, lo // 16 : hi // 16]),
                in1=product[t][:, lo:hi],
                op=ADD,
            )

        def gelu_pair(u, lo, hi, sums):
            base = lo - lo % HALF_S
            nc.scalar.activation(
                out=h_half[lo // HALF_S][:, lo - base : hi - base, 2 * u : 2 * u + 2],
                in_=sums.rearrange("p e s -> p s e"),
                func=GELU,
            )

        def gelu_quad(lo, hi):
            nc.scalar.activation(
                out=h_half[0][:, lo:hi, :].rearrange("p (g i) t -> p g t i", i=4),
                in_=summed[:, :, lo:hi].rearrange("p t (g i) -> p g t i", i=4),
                func=GELU,
            )

        nc.vector.tensor_copy(
            out=pe_picked[:, 0 : HALF_S - LAST], in_=pe_plane[0][:].indirect(offsets[:, HALF_S // 16 : (S - LAST) // 16])
        )
        for lo in range(0, HALF_S, CHUNK):
            gather_add(0, lo, lo + CHUNK, summed[:, 0, lo : lo + CHUNK])
        gather_add(1, HALF_S, S, summed[:, 1, HALF_S:S])
        nc.vector.tensor_tensor(out=summed[:, 0, HALF_S:S], in0=kept_in_psum[:], in1=pe_picked[:], op=ADD)
        gather_add(1, 0, HALF_S, summed[:, 1, 0:HALF_S])
        gelu_pair(0, HALF_S, S, summed[:, 0:2, HALF_S:S])
        gelu_pair(0, CHUNK, HALF_S, summed[:, 0:2, CHUNK:HALF_S])
        gather_add(2, 0, HALF_S, summed[:, 2, 0:HALF_S])
        for lo in range(0, HALF_S, CHUNK):
            gather_add(3, lo, lo + CHUNK, summed[:, 3, lo : lo + CHUNK])
        gelu_quad(0, CHUNK)
        gelu_pair(1, CHUNK, HALF_S, summed[:, 2:4, CHUNK:HALF_S])
        for lo, cuts in ((0, (0, CHUNK)), (CHUNK, (CHUNK, CHUNK + LAST, HALF_S))):
            gather_add(2, HALF_S + lo, HALF_S + lo + CHUNK, late[:, 0, lo : lo + CHUNK])
            for a, b in zip(cuts, cuts[1:]):
                gather_add(3, HALF_S + a, HALF_S + b, late[:, 1, a:b])
                gelu_pair(1, HALF_S + a, HALF_S + b, late[:, :, a:b])

        h_codes = keep.tile([P, S], U32, name="h_codes", tag="pe_plane2", align_bytes=64)
        h_scales = keep.tile([P, S], U8, name="h_scales", align_bytes=64)
        for cuts, copy in (
            ((0, 128), nc.scalar.copy),
            ((128, 256), nc.vector.tensor_copy),
            ((256, 384), nc.scalar.copy),
            ((384, S - LAST, S), nc.vector.tensor_copy),
        ):
            for a, b in zip(cuts, cuts[1:]):
                nc.vector.quantize_mx(
                    out=h_codes[:, a:b].bitcast(FP8X4),
                    scales=h_scales[:, a:b],
                    in_=h_half[a // HALF_S][:, a % HALF_S : a % HALF_S + b - a, :].rearrange("p s t -> p (s t)"),
                )
            lo, hi = cuts[0], cuts[-1]
            acc = psum.tile([P, hi - lo], F32, name="acc%d" % lo, tag="bank%d" % (lo // CHUNK + 1))
            nc.tensor.matmul_mx(
                out=acc[:],
                lhsT=w2_codes[:].bitcast(FP4X4),
                lhsT_scale=w2_plane[:],
                rhs=h_codes[:, lo:hi].bitcast(FP8X4),
                rhs_scale=h_scales[:, lo:hi],
                start=True,
                stop=True,
            )
            result = keep.tile([P, hi - lo], F32, name="result%d" % lo)
            copy(out=result[:], in_=acc[:])
            nc.sync.dma_start(out=out[:, lo:hi], in_=result[:])
